import numpy as np
import ml_dtypes


def mxq(x, axis, fmt="e4m3"):
    dtype, down = {"e4m3": (ml_dtypes.float8_e4m3fn, 7), "e5m2": (ml_dtypes.float8_e5m2, 14)}[fmt]
    v = np.moveaxis(np.asarray(x, np.float32).astype(ml_dtypes.bfloat16).astype(np.float64), axis, -1)
    blocks = v.reshape(v.shape[:-1] + (-1, 32))
    amax = np.abs(blocks).max(-1, keepdims=True)
    byte = np.maximum(np.where(amax > 0, np.frexp(amax)[1] - 1 + 127, 0) - down, 1)
    scale = np.exp2(byte - 127.0)
    codes = (blocks / scale).astype(np.float32).astype(dtype).astype(np.float64)
    return np.moveaxis((codes * scale).reshape(v.shape), -1, axis)


WIDE = False


def mx_kscale(k):
    if not WIDE:
        return np.ones(k)
    levels = np.array([10, -10, 5, -5, 0])
    if k % 512:
        return np.exp2(np.random.permutation(np.resize(levels, k // 32))).repeat(32)
    a = np.empty((k // 512, 16))
    for p in range(k // 512):
        a[p, :8] = np.random.permutation(np.resize(levels, 8))
        for g in range(8):
            far = levels[np.abs(levels - a[p, g]) >= 10]
            a[p, g + 8] = far[np.random.randint(len(far))]
    return np.exp2(a.ravel()).repeat(32)


def f64(x):
    return np.asarray(x).astype(np.float64)


def striped(idx):
    return np.tile(np.asarray(idx).reshape(-1, 16).T, (8, 1)).astype(np.uint16)


def unstriped(offs):
    return offs[:16].T.reshape(-1).astype(np.int64)


E2M1 = np.array([0.0, 0.5, 1.0, 1.5, 2.0, 3.0, 4.0, 6.0, -0.0, -0.5, -1.0, -1.5, -2.0, -3.0, -4.0, -6.0])


def pack_weight(w, fmt):
    k, n = w.shape
    w = f64(np.asarray(w, np.float32).astype(ml_dtypes.bfloat16)).reshape(k // 32, 32, n)
    amax = np.abs(w).max(1)
    if fmt == "e4m3":
        byte = np.frexp(amax)[1] - 1 + 127 - 7
    else:
        mant, ex = np.frexp(amax / 6.0)
        byte = np.where(mant > 0.5, ex, ex - 1) + 127
    byte = np.clip(np.where(amax > 0, byte, 1), 1, 254)
    scaled = (w * np.exp2(127.0 - byte)[:, None, :]).reshape(k, n).astype(np.float32)
    by_word = np.ascontiguousarray(scaled.reshape(k // 512, 128, 4, n).transpose(0, 1, 3, 2))
    if fmt == "e4m3":
        words = by_word.astype(ml_dtypes.float8_e4m3fn).view(np.uint8)
    else:
        c = by_word.astype(ml_dtypes.float4_e2m1fn).view(np.uint8) & 0xF
        words = (c[..., 0::2] | (c[..., 1::2] << 4)).reshape(k // 512, 128, 2 * n)
    return np.ascontiguousarray(words), np.ascontiguousarray(byte.astype(np.uint8).reshape(k // 512, 16, n))


def unpack_weight(words, scales, fmt):
    g, _, n = scales.shape
    words = np.ascontiguousarray(words).reshape(g, 128, n, -1)
    if fmt == "e4m3":
        vals = words.view(ml_dtypes.float8_e4m3fn).astype(np.float64)
    else:
        nib = np.empty((g, 128, n, 4), np.uint8)
        nib[..., 0::2] = words & 0xF
        nib[..., 1::2] = words >> 4
        vals = E2M1[nib]
    vals = vals * np.repeat(np.exp2(scales.astype(np.float64) - 127.0), 8, axis=1)[..., None]
    return vals.transpose(0, 1, 3, 2).reshape(g * 512, n)


def sigmoid(v):
    return 1.0 / (1.0 + np.exp(-v))


D, E, T, I, Q, U, G = 512, 512, 2048, 512, 128, 1024, 64


def setup_inputs():
    n = np.random.standard_normal
    idx2 = np.random.permutation(U)[:I]
    idx = np.random.permutation(T)[:I]
    fd = mx_kscale(D)
    fe = mx_kscale(E)
    keysp = pack_weight(n((D, T)) / fd[:, None], "e4m3")
    valsp = pack_weight(n((E, T)) / fe[:, None], "e4m3")
    return {
        "query": (n((D, Q)) * 1.2 / np.sqrt(D) * fd[:, None]).astype(np.float32),
        "query2": (n((D, Q)) * 1.5 / np.sqrt(D) * fd[:, None]).astype(np.float32),
        "keys_words": keysp[0],
        "keys_scales": keysp[1],
        "notes": (n((D, U)) / fd[:, None]).astype(np.float32),
        "lam": (np.random.uniform(-0.8, 0.8, (Q, 1))).astype(np.float32),
        "reserve": (np.random.uniform(20.0, 60.0, (Q, 1))).astype(np.float32),
        "gout": (n((E, Q)) * 1 / np.sqrt(E) * fe[:, None]).astype(np.float32),
        "vals_words": valsp[0],
        "vals_scales": valsp[1],
        "dquery": (n((D, Q)) * 1.0 / np.sqrt(D) * fd[:, None]).astype(np.float32),
        "base": (0.5 * n((Q, T))).astype(np.float32),
        "offs2": striped(idx2),
        "offs": striped(idx),
    }


def reference(query, query2, keys_words, keys_scales, notes, lam, reserve, gout, vals_words, vals_scales, dquery, base, offs2, offs):
    idx2 = unstriped(offs2)
    idx = unstriped(offs)
    keysu = unpack_weight(keys_words, keys_scales, "e4m3")
    valsu = unpack_weight(vals_words, vals_scales, "e4m3")
    queryq = mxq(f64(query), 0, "e4m3")
    keysidxg = keysu[:, idx]
    a = queryq.T @ keysidxg
    dqueryq = mxq(f64(dquery), 0, "e4m3")
    ta = dqueryq.T @ keysidxg
    query2q = mxq(f64(query2), 0, "e4m3")
    notesidx2q = mxq(f64(notes)[:, idx2], 0, "e4m3")
    b = query2q.T @ notesidx2q
    g1 = sigmoid(b)
    s = a * g1 + (1.0 - g1) * f64(lam)
    p = np.exp(s)
    pg = p.reshape(Q, G, I // G).sum(axis=2)
    pr = np.repeat(pg, I // G, axis=1)
    r = p / (pr - p)
    goutq = mxq(f64(gout), 0, "e4m3")
    valsidxg = valsu[:, idx]
    c0 = goutq.T @ valsidxg
    dr = c0 / (np.sum(r, axis=1, keepdims=True) + f64(reserve)) + np.sum(c0 * r / np.square(np.sum(r, axis=1, keepdims=True) + f64(reserve)) * (-1.0), axis=1, keepdims=True)
    dpr = dr * p / np.square(pr - p) * (-1.0)
    dpg = dpr.reshape(Q, G, I // G).sum(axis=2)
    r1 = np.repeat(dpg, I // G, axis=1)
    dp = dr / (pr - p) + dr * p / np.square(pr - p) + r1
    ts = ta * g1
    tp = ts * p
    tpg = tp.reshape(Q, G, I // G).sum(axis=2)
    tpr = np.repeat(tpg, I // G, axis=1)
    tr = (tp - (tpr - tp) * p / (pr - p)) / (pr - p)
    tdr = np.sum(tr, axis=1, keepdims=True) * c0 / np.square(np.sum(r, axis=1, keepdims=True) + f64(reserve)) * (-1.0) + np.sum((tr * c0 - np.sum(tr, axis=1, keepdims=True) * (np.sum(r, axis=1, keepdims=True) + f64(reserve)) * 2.0 * c0 * r / np.square(np.sum(r, axis=1, keepdims=True) + f64(reserve))) / np.square(np.sum(r, axis=1, keepdims=True) + f64(reserve)) * (-1.0), axis=1, keepdims=True)
    tdpr = (tdr * p + tp * dr - (tpr - tp) * (pr - p) * 2.0 * dr * p / np.square(pr - p)) / np.square(pr - p) * (-1.0)
    tdpg = tdpr.reshape(Q, G, I // G).sum(axis=2)
    tr1 = np.repeat(tdpg, I // G, axis=1)
    tdp = (tdr - (tpr - tp) * dr / (pr - p)) / (pr - p) + (tdr * p + tp * dr - (tpr - tp) * (pr - p) * 2.0 * dr * p / np.square(pr - p)) / np.square(pr - p) + tr1
    tds = tdp * p + tp * dp
    tda = tds * g1
    gs = tda * 512.0
    gf = np.zeros((Q, T))
    gf[:, idx] = gs
    y = f64(base) + gf
    return y

@@ -1,0 +1,265 @@
+from contextlib import ExitStack
+
+import concourse.mybir as mybir
+
+F32 = mybir.dt.float32
+BF16 = mybir.dt.bfloat16
+I32 = mybir.dt.int32
+U32 = mybir.dt.uint32
+U16 = mybir.dt.uint16
+U8 = mybir.dt.uint8
+FP8X4 = mybir.dt.float8_e4m3fn_x4
+ALU = mybir.AluOpType
+ACT = mybir.ActivationFunctionType
+AXIS_X = mybir.AxisListType.X
+
+P = 128
+PACK = 4
+D, E, T, I, Q, U, G = 512, 512, 2048, 512, 128, 1024, 64
+RUN = I // G
+HALF = I // 2
+PER_COLUMN = 16
+OUT_CHUNK = 512
+
+FLOPS = 2 * Q * I * (3 * D + E)
+
+VECTOR_SLOTS = (192, 192, 192, 320)
+VECTOR_WEAVE = 352
+
+
+def tile_attend_hvtilted_oddsof_s_kernel(tc, query, query2, keys_words, keys_scales, notes, lam, reserve, gout,
+                                          vals_words, vals_scales, dquery, base, offs2, offs, out):
+    nc = tc.nc
+    with ExitStack() as ctx:
+        lists = ctx.enter_context(tc.tile_pool(name="lists", bufs=1))
+        sb = ctx.enter_context(tc.tile_pool(name="sb", bufs=1))
+        ps = ctx.enter_context(tc.psum_pool(name="ps", bufs=1))
+
+        def wide(name, dtype=F32, columns=I, tag=None):
+            return sb.tile([P, columns], dtype, name=name, tag=tag or name, align_bytes=64)
+
+        def column(name):
+            return sb.tile([P, 1], F32, name=name)
+
+        halves = [slice(h * HALF, (h + 1) * HALF) for h in range(2)]
+        run_halves = [slice(h * G // 2, (h + 1) * G // 2) for h in range(2)]
+
+        def by_run(ap):
+            return ap.rearrange("p (g j) -> p g j", j=RUN)
+
+        def spread(ap):
+            return ap.unsqueeze(2).to_broadcast([P, ap.shape[1], RUN])
+
+        key_scale_pool = wide("key_scale_pool", U8, T)
+        val_scale_pool = wide("val_scale_pool", U8, T)
+        placed = wide("placed", F32, T)
+        nc.vector.memset(key_scale_pool[:].bitcast(I32), 0)
+        nc.vector.memset(val_scale_pool[:].bitcast(I32), 0)
+        nc.vector.memset(placed[:], 0.0)
+        consts = sb.tile([P, 4], F32, name="consts")
+        for j, value in enumerate((0.5, 1.0, -0.5, -0.25)):
+            nc.gpsimd.memset(consts[:, j:j + 1], value)
+        half_c, one_c, minus_half_c, minus_quarter_c = (consts[:, j:j + 1] for j in range(4))
+
+        note_list = lists.tile([P, I // PER_COLUMN], U16, name="note_list")
+        token_list = lists.tile([P, I // PER_COLUMN], U16, name="token_list")
+        nc.sync.dma_start(note_list[:], offs2)
+
+        def load_rows(name, src):
+            raw = sb.tile([P, PACK, Q], F32, name=name)
+            nc.sync.dma_start(raw[:], src.rearrange("(p j) w -> p j w", j=PACK))
+            return raw
+
+        def load_scales(queue, pool_tile, src):
+            rows = src[0].bitcast(I32)
+            for quad in range(4):
+                queue.dma_start(pool_tile[32 * quad:32 * quad + 4, :].bitcast(I32), rows[4 * quad:4 * quad + 4, :])
+
+        def load_words(name, src):
+            words = wide(name, I32, T)
+            nc.sync.dma_start(words[:], src[0].rearrange("p n t -> p (n t)").bitcast(I32))
+            return words
+
+        load_scales(nc.scalar, key_scale_pool, keys_scales)
+        load_scales(nc.gpsimd, val_scale_pool, vals_scales)
+        note_rows = notes.rearrange("(p j) u -> j p u", j=PACK)
+        note_planes = []
+        for t in range(PACK):
+            plane = wide("note_plane%d" % t, F32, U)
+            nc.sync.dma_start(plane[:], note_rows[t])
+            note_planes.append(plane)
+            if t == 0:
+                nc.sync.dma_start(token_list[:], offs)
+        query2_raw = load_rows("query2_raw", query2)
+        query_raw = load_rows("query_raw", query)
+        dquery_raw = load_rows("dquery_raw", dquery)
+        key_word_pool = load_words("key_word_pool", keys_words)
+        lam_c = column("lam_c")
+        nc.sync.dma_start(lam_c[:], lam)
+        gout_raw = load_rows("gout_raw", gout)
+        val_word_pool = load_words("val_word_pool", vals_words)
+        reserve_c = column("reserve_c")
+        nc.sync.dma_start(reserve_c[:], reserve)
+        base_chunks = []
+        for j in range(T // OUT_CHUNK):
+            chunk = wide("base%d" % j, F32, OUT_CHUNK)
+            nc.sync.dma_start(chunk[:], base[:, j * OUT_CHUNK:(j + 1) * OUT_CHUNK])
+            base_chunks.append(chunk)
+
+        note_g = sb.tile([P, PACK, I], BF16, name="note_g", align_bytes=64)
+        key_scales = wide("key_scales", U8)
+        val_scales = wide("val_scales", U8)
+        for t in range(PACK):
+            cut = VECTOR_SLOTS[t]
+            nc.vector.tensor_copy(note_g[:, t, :cut], note_planes[t][:].indirect(note_list[:, :cut // PER_COLUMN]))
+            nc.scalar.activation(note_g[:, t, cut:], note_planes[t][:].indirect(note_list[:, cut // PER_COLUMN:]), ACT.Copy)
+            if t == 1:
+                nc.vector.tensor_copy(key_scales[:], key_scale_pool[:].indirect(token_list[:]))
+
+        def weave(engine_copy, dst, src):
+            engine_copy(dst.rearrange("p (c i) t -> p c t i", i=4), src.rearrange("p t (c i) -> p c t i", i=4))
+
+        def quantise(name, grouped, columns):
+            codes = wide(name + "_codes", U32, columns)
+            scales = wide(name + "_scales", U8, columns)
+            nc.vector.quantize_mx(out=codes[:].bitcast(FP8X4), scales=scales[:], in_=grouped.rearrange("p w j -> p (w j)"))
+            return codes, scales
+
+        note_w = sb.tile([P, I, PACK], BF16, name="note_w", align_bytes=64)
+        weave(nc.vector.tensor_copy, note_w[:, :VECTOR_WEAVE, :], note_g[:, :, :VECTOR_WEAVE])
+        weave(nc.scalar.copy, note_w[:, VECTOR_WEAVE:, :], note_g[:, :, VECTOR_WEAVE:])
+        note_codes, note_scales = quantise("note", note_w[:], I)
+
+        query2_w = sb.tile([P, Q, PACK], BF16, name="query2_w", align_bytes=64)
+        weave(nc.scalar.copy, query2_w[:], query2_raw[:])
+        query2_codes, query2_scales = quantise("query2", query2_w[:], Q)
+
+        def product(name, rows, row_columns, codes, scales):
+            bank = ps.tile([Q, codes.shape[1]], F32, name=name)
+            nc.tensor.matmul_mx(out=bank[:], lhsT=rows[0][:, row_columns].bitcast(FP8X4), lhsT_scale=rows[1][:, row_columns],
+                                rhs=codes.bitcast(FP8X4), rhs_scale=scales, start=True, stop=True)
+            return bank
+
+        b_bank = product("b_bank", (query2_codes, query2_scales), slice(0, Q), note_codes[:], note_scales[:])
+
+        nc.vector.tensor_copy(val_scales[:], val_scale_pool[:].indirect(token_list[:]))
+        pair_w = sb.tile([P, 2 * Q, PACK], BF16, name="pair_w", align_bytes=64)
+        weave(nc.scalar.copy, pair_w[:, :Q, :], query_raw[:])
+        weave(nc.scalar.copy, pair_w[:, Q:, :], dquery_raw[:])
+        pair = quantise("pair", pair_w[:], 2 * Q)
+
+        tanh_b = wide("tanh_b")
+        gate = wide("gate")
+        nc.scalar.activation(tanh_b[:], b_bank[:], ACT.Tanh, scale=0.5)
+        nc.scalar.activation(gate[:], tanh_b[:], ACT.Identity, bias=half_c, scale=0.5)
+
+        key_words = wide("key_words", U32)
+        a_banks = []
+        for h in range(2):
+            nc.vector.tensor_copy(key_words[:, halves[h]],
+                                  key_word_pool[:].bitcast(U32).indirect(token_list[:, h * HALF // PER_COLUMN:(h + 1) * HALF // PER_COLUMN]))
+            a_banks.append(product("a_bank%d" % h, pair, slice(0, Q), key_words[:, halves[h]], key_scales[:, halves[h]]))
+        ta_bank = product("ta_bank", pair, slice(Q, 2 * Q), key_words[:], key_scales[:])
+
+        gout_w = sb.tile([P, Q, PACK], BF16, name="gout_w", align_bytes=64)
+        weave(nc.scalar.copy, gout_w[:], gout_raw[:])
+
+        score = wide("score")
+        p = wide("p")
+        for h in range(2):
+            nc.vector.scalar_tensor_tensor(score[:, halves[h]], a_banks[h][:], lam_c[:], gate[:, halves[h]], ALU.subtract, ALU.mult)
+            nc.scalar.activation(p[:, halves[h]], score[:, halves[h]], ACT.Exp, bias=lam_c[:])
+        ts = wide("ts")
+        nc.vector.tensor_tensor(ts[:], ta_bank[:], gate[:], ALU.mult)
+        gout_q = quantise("gout", gout_w[:], Q)
+        p_run = wide("p_run", F32, G)
+        nc.vector.tensor_reduce(p_run[:], by_run(p[:]), AXIS_X, ALU.add)
+        val_words = wide("val_words", U32)
+        nc.vector.tensor_copy(val_words[:], val_word_pool[:].bitcast(U32).indirect(token_list[:]))
+        c_bank = product("c_bank", gout_q, slice(0, Q), val_words[:], val_scales[:])
+        inv_run = wide("inv_run", F32, G, tag="val_word_pool")
+        nc.vector.reciprocal(inv_run[:], p_run[:])
+        reserve_less = column("reserve_less")
+        nc.vector.tensor_scalar(reserve_less[:], reserve_c[:], float(I), None, ALU.subtract)
+
+        share = wide("share")
+        weighted = wide("weighted")
+        ts_mean = wide("ts_mean", F32, G)
+        z = wide("z")
+        for h in range(2):
+            nc.vector.tensor_tensor(by_run(share[:, halves[h]]), by_run(p[:, halves[h]]), spread(inv_run[:, run_halves[h]]), ALU.mult)
+        root = wide("root")
+        u = wide("u")
+        u_sum = column("u_sum")
+        k_plus = wide("k_plus")
+        k = wide("k")
+        total = column("total")
+        nc.scalar.activation(root[:], share[:], ACT.Abs_reciprocal_sqrt, bias=one_c, scale=-1.0)
+        nc.scalar.activation(u[:], root[:], ACT.Square, accum_out=u_sum[:])
+        nc.scalar.activation(total[:], u_sum[:], ACT.Identity, bias=reserve_less[:])
+        nc.scalar.activation(k_plus[:], u[:], ACT.Square, bias=minus_half_c)
+        nc.scalar.activation(k[:], k_plus[:], ACT.Identity, bias=minus_quarter_c)
+        for h in range(2):
+            nc.vector.tensor_tensor(weighted[:, halves[h]], share[:, halves[h]], ts[:, halves[h]], ALU.mult)
+        for h in range(2):
+            nc.vector.tensor_reduce(ts_mean[:, run_halves[h]], by_run(weighted[:, halves[h]]), AXIS_X, ALU.add)
+        for h in range(2):
+            nc.vector.tensor_tensor(by_run(z[:, halves[h]]), by_run(ts[:, halves[h]]), spread(ts_mean[:, run_halves[h]]), ALU.subtract)
+
+        cr = wide("cr")
+        cr_sum = column("cr_sum")
+        inv_total = column("inv_total")
+        nc.vector.reciprocal(inv_total[:], total[:])
+        nc.vector.scalar_tensor_tensor(cr[:], u[:], 1.0, c_bank[:], ALU.subtract, ALU.mult, accum_out=cr_sum[:])
+        c_mean = column("c_mean")
+        nc.scalar.activation(c_mean[:], cr_sum[:], ACT.Copy, scale=inv_total[:])
+        tr = wide("tr")
+        tr_sum = column("tr_sum")
+        nc.vector.scalar_tensor_tensor(tr[:], k_plus[:], 0.25, z[:], ALU.subtract, ALU.mult, accum_out=tr_sum[:])
+        half_inv = column("half_inv")
+        nc.scalar.activation(half_inv[:], inv_total[:], ACT.Copy, scale=0.5)
+        kappa = column("kappa")
+        nc.scalar.activation(kappa[:], tr_sum[:], ACT.Copy, scale=half_inv[:])
+        n_half = wide("n_half")
+        nc.vector.scalar_tensor_tensor(n_half[:], u[:], 0.5, z[:], ALU.subtract, ALU.mult)
+        dk = wide("dk")
+        dk_run = wide("dk_run", F32, G)
+        for h in range(2):
+            nc.vector.scalar_tensor_tensor(dk[:, halves[h]], c_bank[:, halves[h]], c_mean[:], k[:, halves[h]], ALU.subtract, ALU.mult)
+        for h in range(2):
+            nc.vector.tensor_reduce(dk_run[:, run_halves[h]], by_run(dk[:, halves[h]]), AXIS_X, ALU.add)
+        dz = wide("dz")
+        dz_sum = column("dz_sum")
+        nc.vector.scalar_tensor_tensor(dz[:], dk[:], 0.5, z[:], ALU.mult, ALU.mult, accum_out=dz_sum[:])
+        delta = column("delta")
+        nc.scalar.activation(delta[:], dz_sum[:], ACT.Copy, scale=inv_total[:])
+        out_scale = column("out_scale")
+        nc.scalar.activation(out_scale[:], inv_total[:], ACT.Copy, scale=-1024.0)
+        gate_scaled = wide("gate_scaled")
+        nc.scalar.activation(gate_scaled[:], gate[:], ACT.Copy, scale=out_scale[:])
+        t2 = wide("t2")
+        nc.vector.scalar_tensor_tensor(t2[:], n_half[:], kappa[:], dk[:], ALU.subtract, ALU.mult)
+        e = wide("e")
+        nc.vector.scalar_tensor_tensor(by_run(e[:]), by_run(z[:]), 0.5, spread(dk_run[:]), ALU.mult, ALU.mult)
+        bn = wide("bn")
+        bn_run = wide("bn_run", F32, G)
+        e2 = wide("e2")
+        e3 = wide("e3")
+        fn = wide("fn")
+        for h in range(2):
+            nc.vector.scalar_tensor_tensor(bn[:, halves[h]], k[:, halves[h]], delta[:], t2[:, halves[h]], ALU.mult, ALU.subtract)
+        for h in range(2):
+            nc.vector.tensor_reduce(bn_run[:, run_halves[h]], by_run(bn[:, halves[h]]), AXIS_X, ALU.add)
+        for h in range(2):
+            nc.vector.tensor_tensor(by_run(e2[:, halves[h]]), by_run(e[:, halves[h]]), spread(bn_run[:, run_halves[h]]), ALU.subtract)
+        for h in range(2):
+            nc.vector.tensor_tensor(e3[:, halves[h]], e2[:, halves[h]], share[:, halves[h]], ALU.mult)
+        for h in range(2):
+            nc.vector.tensor_tensor(fn[:, halves[h]], e3[:, halves[h]], bn[:, halves[h]], ALU.add)
+
+        nc.vector.tensor_tensor(placed[:].indirect(token_list[:]), fn[:], gate_scaled[:], ALU.mult)
+        for j in range(T // OUT_CHUNK):
+            cols = slice(j * OUT_CHUNK, (j + 1) * OUT_CHUNK)
+            result = wide("result%d" % j, F32, OUT_CHUNK)
+            nc.vector.tensor_tensor(result[:], placed[:, cols], base_chunks[j][:], ALU.add)
+            nc.sync.dma_start(out[:, cols], result[:])

@@ -19,12 +19,11 @@ D, E, T, I, Q, U, G = 512, 512, 2048, 512, 128, 1024, 64
 RUN = I // G
 HALF = I // 2
 PER_COLUMN = 16
-OUT_CHUNK = 512
+OUT_CHUNKS = (640, 576, 512, 320)
 
 FLOPS = 2 * Q * I * (3 * D + E)
 
-VECTOR_SLOTS = (192, 192, 192, 320)
-VECTOR_WEAVE = 352
+VECTOR_SLOTS = 352
 
 
 def tile_attend_hvtilted_oddsof_s_kernel(tc, query, query2, keys_words, keys_scales, notes, lam, reserve, gout,
@@ -43,6 +42,7 @@ def tile_attend_hvtilted_oddsof_s_kernel(tc, query, query2, keys_words, keys_sca
 
         halves = [slice(h * HALF, (h + 1) * HALF) for h in range(2)]
         run_halves = [slice(h * G // 2, (h + 1) * G // 2) for h in range(2)]
+        list_halves = [slice(h * HALF // PER_COLUMN, (h + 1) * HALF // PER_COLUMN) for h in range(2)]
 
         def by_run(ap):
             return ap.rearrange("p (g j) -> p g j", j=RUN)
@@ -63,58 +63,49 @@ def tile_attend_hvtilted_oddsof_s_kernel(tc, query, query2, keys_words, keys_sca
 
         note_list = lists.tile([P, I // PER_COLUMN], U16, name="note_list")
         token_list = lists.tile([P, I // PER_COLUMN], U16, name="token_list")
-        nc.sync.dma_start(note_list[:], offs2)
 
         def load_rows(name, src):
             raw = sb.tile([P, PACK, Q], F32, name=name)
             nc.sync.dma_start(raw[:], src.rearrange("(p j) w -> p j w", j=PACK))
             return raw
 
-        def load_scales(queue, pool_tile, src):
-            rows = src[0].bitcast(I32)
-            for quad in range(4):
-                queue.dma_start(pool_tile[32 * quad:32 * quad + 4, :].bitcast(I32), rows[4 * quad:4 * quad + 4, :])
-
         def load_words(name, src):
             words = wide(name, I32, T)
             nc.sync.dma_start(words[:], src[0].rearrange("p n t -> p (n t)").bitcast(I32))
             return words
 
-        load_scales(nc.scalar, key_scale_pool, keys_scales)
-        load_scales(nc.gpsimd, val_scale_pool, vals_scales)
+        def load_column(name, src):
+            tile = column(name)
+            nc.sync.dma_start(tile[:], src)
+            return tile
+
         note_rows = notes.rearrange("(p j) u -> j p u", j=PACK)
-        note_planes = []
-        for t in range(PACK):
+
+        def load_note_plane(t):
             plane = wide("note_plane%d" % t, F32, U)
             nc.sync.dma_start(plane[:], note_rows[t])
-            note_planes.append(plane)
-            if t == 0:
-                nc.sync.dma_start(token_list[:], offs)
+            return plane
+
+        def load_scales(pool_tile, src):
+            rows = src[0].bitcast(I32)
+            for r in range(4):
+                nc.sync.dma_start(pool_tile[r:P:32, :].bitcast(I32), rows[r:16:4, :])
+
+        nc.sync.dma_start(note_list[:], offs2)
+        nc.sync.dma_start(token_list[:], offs)
+        note_planes = [load_note_plane(t) for t in range(PACK)]
         query2_raw = load_rows("query2_raw", query2)
         query_raw = load_rows("query_raw", query)
-        dquery_raw = load_rows("dquery_raw", dquery)
+        load_scales(key_scale_pool, keys_scales)
         key_word_pool = load_words("key_word_pool", keys_words)
-        lam_c = column("lam_c")
-        nc.sync.dma_start(lam_c[:], lam)
+        load_scales(val_scale_pool, vals_scales)
+        lam_c = load_column("lam_c", lam)
+        dquery_raw = load_rows("dquery_raw", dquery)
         gout_raw = load_rows("gout_raw", gout)
         val_word_pool = load_words("val_word_pool", vals_words)
-        reserve_c = column("reserve_c")
-        nc.sync.dma_start(reserve_c[:], reserve)
-        base_chunks = []
-        for j in range(T // OUT_CHUNK):
-            chunk = wide("base%d" % j, F32, OUT_CHUNK)
-            nc.sync.dma_start(chunk[:], base[:, j * OUT_CHUNK:(j + 1) * OUT_CHUNK])
-            base_chunks.append(chunk)
-
-        note_g = sb.tile([P, PACK, I], BF16, name="note_g", align_bytes=64)
-        key_scales = wide("key_scales", U8)
-        val_scales = wide("val_scales", U8)
-        for t in range(PACK):
-            cut = VECTOR_SLOTS[t]
-            nc.vector.tensor_copy(note_g[:, t, :cut], note_planes[t][:].indirect(note_list[:, :cut // PER_COLUMN]))
-            nc.scalar.activation(note_g[:, t, cut:], note_planes[t][:].indirect(note_list[:, cut // PER_COLUMN:]), ACT.Copy)
-            if t == 1:
-                nc.vector.tensor_copy(key_scales[:], key_scale_pool[:].indirect(token_list[:]))
+        reserve_c = load_column("reserve_c", reserve)
+        base_sb = wide("base_sb", F32, T)
+        nc.sync.dma_start(base_sb[:], base)
 
         def weave(engine_copy, dst, src):
             engine_copy(dst.rearrange("p (c i) t -> p c t i", i=4), src.rearrange("p t (c i) -> p c t i", i=4))
@@ -125,69 +116,71 @@ def tile_attend_hvtilted_oddsof_s_kernel(tc, query, query2, keys_words, keys_sca
             nc.vector.quantize_mx(out=codes[:].bitcast(FP8X4), scales=scales[:], in_=grouped.rearrange("p w j -> p (w j)"))
             return codes, scales
 
-        note_w = sb.tile([P, I, PACK], BF16, name="note_w", align_bytes=64)
-        weave(nc.vector.tensor_copy, note_w[:, :VECTOR_WEAVE, :], note_g[:, :, :VECTOR_WEAVE])
-        weave(nc.scalar.copy, note_w[:, VECTOR_WEAVE:, :], note_g[:, :, VECTOR_WEAVE:])
-        note_codes, note_scales = quantise("note", note_w[:], I)
+        def gpsimd_round(dst, src):
+            nc.gpsimd.tensor_scalar(dst, src, 1.0, 0.0, ALU.mult, ALU.add)
 
-        query2_w = sb.tile([P, Q, PACK], BF16, name="query2_w", align_bytes=64)
-        weave(nc.scalar.copy, query2_w[:], query2_raw[:])
-        query2_codes, query2_scales = quantise("query2", query2_w[:], Q)
+        def weave_rows(name, engine_copy, raw):
+            woven = sb.tile([P, Q, PACK], BF16, name=name, align_bytes=64)
+            weave(engine_copy, woven[:], raw[:])
+            return woven
 
-        def product(name, rows, row_columns, codes, scales):
+        def product(name, rows, codes, scales):
             bank = ps.tile([Q, codes.shape[1]], F32, name=name)
-            nc.tensor.matmul_mx(out=bank[:], lhsT=rows[0][:, row_columns].bitcast(FP8X4), lhsT_scale=rows[1][:, row_columns],
+            nc.tensor.matmul_mx(out=bank[:], lhsT=rows[0][:].bitcast(FP8X4), lhsT_scale=rows[1][:],
                                 rhs=codes.bitcast(FP8X4), rhs_scale=scales, start=True, stop=True)
             return bank
 
-        b_bank = product("b_bank", (query2_codes, query2_scales), slice(0, Q), note_codes[:], note_scales[:])
-
-        nc.vector.tensor_copy(val_scales[:], val_scale_pool[:].indirect(token_list[:]))
-        pair_w = sb.tile([P, 2 * Q, PACK], BF16, name="pair_w", align_bytes=64)
-        weave(nc.scalar.copy, pair_w[:, :Q, :], query_raw[:])
-        weave(nc.scalar.copy, pair_w[:, Q:, :], dquery_raw[:])
-        pair = quantise("pair", pair_w[:], 2 * Q)
+        note_w = sb.tile([P, I, PACK], BF16, name="note_w", align_bytes=64)
+        note_g = sb.tile([P, PACK, I - VECTOR_SLOTS], BF16, name="note_g", align_bytes=64)
+        cut = VECTOR_SLOTS // PER_COLUMN
+        for t in range(PACK):
+            nc.vector.tensor_copy(note_w[:, :VECTOR_SLOTS, t], note_planes[t][:].indirect(note_list[:, :cut]))
+            nc.scalar.activation(note_g[:, t, :], note_planes[t][:].indirect(note_list[:, cut:]), ACT.Copy)
+        weave(nc.scalar.copy, note_w[:, VECTOR_SLOTS:, :], note_g[:])
+        query2_w = weave_rows("query2_w", nc.scalar.copy, query2_raw)
+        note_codes, note_scales = quantise("note", note_w[:], I)
+        query2_q = quantise("query2", query2_w[:], Q)
+        b_bank = product("b_bank", query2_q, note_codes[:], note_scales[:])
+        query_w = weave_rows("query_w", nc.scalar.copy, query_raw)
+        key_scales = wide("key_scales", U8)
+        nc.vector.tensor_copy(key_scales[:], key_scale_pool[:].indirect(token_list[:]))
+        query_q = quantise("query", query_w[:], Q)
 
         tanh_b = wide("tanh_b")
         gate = wide("gate")
-        nc.scalar.activation(tanh_b[:], b_bank[:], ACT.Tanh, scale=0.5)
-        nc.scalar.activation(gate[:], tanh_b[:], ACT.Identity, bias=half_c, scale=0.5)
+        for h in range(2):
+            nc.scalar.activation(tanh_b[:, halves[h]], b_bank[:, halves[h]], ACT.Tanh, scale=0.5)
+            nc.scalar.activation(gate[:, halves[h]], tanh_b[:, halves[h]], ACT.Identity, bias=half_c, scale=0.5)
 
         key_words = wide("key_words", U32)
         a_banks = []
         for h in range(2):
-            nc.vector.tensor_copy(key_words[:, halves[h]],
-                                  key_word_pool[:].bitcast(U32).indirect(token_list[:, h * HALF // PER_COLUMN:(h + 1) * HALF // PER_COLUMN]))
-            a_banks.append(product("a_bank%d" % h, pair, slice(0, Q), key_words[:, halves[h]], key_scales[:, halves[h]]))
-        ta_bank = product("ta_bank", pair, slice(Q, 2 * Q), key_words[:], key_scales[:])
+            nc.vector.tensor_copy(key_words[:, halves[h]], key_word_pool[:].bitcast(U32).indirect(token_list[:, list_halves[h]]))
+            a_banks.append(product("a_bank%d" % h, query_q, key_words[:, halves[h]], key_scales[:, halves[h]]))
 
-        gout_w = sb.tile([P, Q, PACK], BF16, name="gout_w", align_bytes=64)
-        weave(nc.scalar.copy, gout_w[:], gout_raw[:])
+        dquery_w = weave_rows("dquery_w", gpsimd_round, dquery_raw)
+        gout_w = weave_rows("gout_w", gpsimd_round, gout_raw)
+        reserve_less = column("reserve_less")
+        nc.gpsimd.tensor_scalar(reserve_less[:], reserve_c[:], 1.0, -float(I), ALU.mult, ALU.add)
 
         score = wide("score")
         p = wide("p")
+        p_run = wide("p_run", F32, G)
         for h in range(2):
             nc.vector.scalar_tensor_tensor(score[:, halves[h]], a_banks[h][:], lam_c[:], gate[:, halves[h]], ALU.subtract, ALU.mult)
             nc.scalar.activation(p[:, halves[h]], score[:, halves[h]], ACT.Exp, bias=lam_c[:])
-        ts = wide("ts")
-        nc.vector.tensor_tensor(ts[:], ta_bank[:], gate[:], ALU.mult)
-        gout_q = quantise("gout", gout_w[:], Q)
-        p_run = wide("p_run", F32, G)
+        val_scales = wide("val_scales", U8)
+        nc.vector.tensor_copy(val_scales[:], val_scale_pool[:].indirect(token_list[:]))
         nc.vector.tensor_reduce(p_run[:], by_run(p[:]), AXIS_X, ALU.add)
-        val_words = wide("val_words", U32)
-        nc.vector.tensor_copy(val_words[:], val_word_pool[:].bitcast(U32).indirect(token_list[:]))
-        c_bank = product("c_bank", gout_q, slice(0, Q), val_words[:], val_scales[:])
-        inv_run = wide("inv_run", F32, G, tag="val_word_pool")
-        nc.vector.reciprocal(inv_run[:], p_run[:])
-        reserve_less = column("reserve_less")
-        nc.vector.tensor_scalar(reserve_less[:], reserve_c[:], float(I), None, ALU.subtract)
-
+        dquery_q = quantise("dquery", dquery_w[:], Q)
+        ta_bank = product("ta_bank", dquery_q, key_words[:], key_scales[:])
+        inv_run = wide("inv_run", F32, G)
         share = wide("share")
-        weighted = wide("weighted")
-        ts_mean = wide("ts_mean", F32, G)
-        z = wide("z")
+        for h in range(2):
+            nc.vector.reciprocal(inv_run[:, run_halves[h]], p_run[:, run_halves[h]])
         for h in range(2):
             nc.vector.tensor_tensor(by_run(share[:, halves[h]]), by_run(p[:, halves[h]]), spread(inv_run[:, run_halves[h]]), ALU.mult)
+
         root = wide("root")
         u = wide("u")
         u_sum = column("u_sum")
@@ -199,20 +192,68 @@ def tile_attend_hvtilted_oddsof_s_kernel(tc, query, query2, keys_words, keys_sca
         nc.scalar.activation(total[:], u_sum[:], ACT.Identity, bias=reserve_less[:])
         nc.scalar.activation(k_plus[:], u[:], ACT.Square, bias=minus_half_c)
         nc.scalar.activation(k[:], k_plus[:], ACT.Identity, bias=minus_quarter_c)
+
+        ts = wide("ts")
+        nc.vector.tensor_tensor(ts[:], ta_bank[:], gate[:], ALU.mult)
+        gout_q = quantise("gout", gout_w[:], Q)
+        weighted = wide("weighted")
+        val_words = wide("val_words", U32)
+        nc.vector.tensor_copy(val_words[:], val_word_pool[:].bitcast(U32).indirect(token_list[:]))
+        c_bank = product("c_bank", gout_q, val_words[:], val_scales[:])
+        ts_mean = wide("ts_mean", F32, G, tag="val_word_pool")
         for h in range(2):
             nc.vector.tensor_tensor(weighted[:, halves[h]], share[:, halves[h]], ts[:, halves[h]], ALU.mult)
         for h in range(2):
             nc.vector.tensor_reduce(ts_mean[:, run_halves[h]], by_run(weighted[:, halves[h]]), AXIS_X, ALU.add)
-        for h in range(2):
-            nc.vector.tensor_tensor(by_run(z[:, halves[h]]), by_run(ts[:, halves[h]]), spread(ts_mean[:, run_halves[h]]), ALU.subtract)
-
-        cr = wide("cr")
-        cr_sum = column("cr_sum")
         inv_total = column("inv_total")
         nc.vector.reciprocal(inv_total[:], total[:])
+        z = wide("z")
+        for h in range(2):
+            nc.vector.tensor_tensor(by_run(z[:, halves[h]]), by_run(ts[:, halves[h]]), spread(ts_mean[:, run_halves[h]]), ALU.subtract)
+        cr = wide("cr")
+        cr_sum = column("cr_sum")
         nc.vector.scalar_tensor_tensor(cr[:], u[:], 1.0, c_bank[:], ALU.subtract, ALU.mult, accum_out=cr_sum[:])
         c_mean = column("c_mean")
         nc.scalar.activation(c_mean[:], cr_sum[:], ACT.Copy, scale=inv_total[:])
+        n_half = wide("n_half")
+        dk = wide("dk")
+        dk_run = wide("dk_run", F32, G)
+        t2 = wide("t2")
+        e = wide("e")
+        bn = wide("bn")
+        bn_run = wide("bn_run", F32, G)
+        e2 = wide("e2")
+        e3 = wide("e3")
+        fn = wide("fn")
+
+        def step_n(h):
+            nc.vector.scalar_tensor_tensor(n_half[:, halves[h]], u[:, halves[h]], 0.5, z[:, halves[h]], ALU.subtract, ALU.mult)
+
+        def step_dk_run(h):
+            nc.vector.tensor_reduce(dk_run[:, run_halves[h]], by_run(dk[:, halves[h]]), AXIS_X, ALU.add)
+
+        def step_t2(h):
+            nc.vector.scalar_tensor_tensor(t2[:, halves[h]], n_half[:, halves[h]], kappa[:], dk[:, halves[h]], ALU.subtract, ALU.mult)
+
+        def step_e(h):
+            nc.vector.scalar_tensor_tensor(by_run(e[:, halves[h]]), by_run(z[:, halves[h]]), 0.5, spread(dk_run[:, run_halves[h]]), ALU.mult, ALU.mult)
+
+        def step_bn(h):
+            nc.vector.scalar_tensor_tensor(bn[:, halves[h]], k[:, halves[h]], delta[:], t2[:, halves[h]], ALU.mult, ALU.subtract)
+
+        def step_bn_run(h):
+            nc.vector.tensor_reduce(bn_run[:, run_halves[h]], by_run(bn[:, halves[h]]), AXIS_X, ALU.add)
+
+        def step_e2(h):
+            nc.vector.tensor_tensor(by_run(e2[:, halves[h]]), by_run(e[:, halves[h]]), spread(bn_run[:, run_halves[h]]), ALU.subtract)
+
+        def step_e3(h):
+            nc.vector.tensor_tensor(e3[:, halves[h]], e2[:, halves[h]], share[:, halves[h]], ALU.mult)
+
+        def step_fn(h):
+            nc.vector.tensor_tensor(fn[:, halves[h]], e3[:, halves[h]], bn[:, halves[h]], ALU.add)
+
+        step_n(0)
         tr = wide("tr")
         tr_sum = column("tr_sum")
         nc.vector.scalar_tensor_tensor(tr[:], k_plus[:], 0.25, z[:], ALU.subtract, ALU.mult, accum_out=tr_sum[:])
@@ -220,14 +261,9 @@ def tile_attend_hvtilted_oddsof_s_kernel(tc, query, query2, keys_words, keys_sca
         nc.scalar.activation(half_inv[:], inv_total[:], ACT.Copy, scale=0.5)
         kappa = column("kappa")
         nc.scalar.activation(kappa[:], tr_sum[:], ACT.Copy, scale=half_inv[:])
-        n_half = wide("n_half")
-        nc.vector.scalar_tensor_tensor(n_half[:], u[:], 0.5, z[:], ALU.subtract, ALU.mult)
-        dk = wide("dk")
-        dk_run = wide("dk_run", F32, G)
         for h in range(2):
             nc.vector.scalar_tensor_tensor(dk[:, halves[h]], c_bank[:, halves[h]], c_mean[:], k[:, halves[h]], ALU.subtract, ALU.mult)
-        for h in range(2):
-            nc.vector.tensor_reduce(dk_run[:, run_halves[h]], by_run(dk[:, halves[h]]), AXIS_X, ALU.add)
+        step_dk_run(0)
         dz = wide("dz")
         dz_sum = column("dz_sum")
         nc.vector.scalar_tensor_tensor(dz[:], dk[:], 0.5, z[:], ALU.mult, ALU.mult, accum_out=dz_sum[:])
@@ -237,29 +273,32 @@ def tile_attend_hvtilted_oddsof_s_kernel(tc, query, query2, keys_words, keys_sca
         nc.scalar.activation(out_scale[:], inv_total[:], ACT.Copy, scale=-1024.0)
         gate_scaled = wide("gate_scaled")
         nc.scalar.activation(gate_scaled[:], gate[:], ACT.Copy, scale=out_scale[:])
-        t2 = wide("t2")
-        nc.vector.scalar_tensor_tensor(t2[:], n_half[:], kappa[:], dk[:], ALU.subtract, ALU.mult)
-        e = wide("e")
-        nc.vector.scalar_tensor_tensor(by_run(e[:]), by_run(z[:]), 0.5, spread(dk_run[:]), ALU.mult, ALU.mult)
-        bn = wide("bn")
-        bn_run = wide("bn_run", F32, G)
-        e2 = wide("e2")
-        e3 = wide("e3")
-        fn = wide("fn")
-        for h in range(2):
-            nc.vector.scalar_tensor_tensor(bn[:, halves[h]], k[:, halves[h]], delta[:], t2[:, halves[h]], ALU.mult, ALU.subtract)
-        for h in range(2):
-            nc.vector.tensor_reduce(bn_run[:, run_halves[h]], by_run(bn[:, halves[h]]), AXIS_X, ALU.add)
-        for h in range(2):
-            nc.vector.tensor_tensor(by_run(e2[:, halves[h]]), by_run(e[:, halves[h]]), spread(bn_run[:, run_halves[h]]), ALU.subtract)
-        for h in range(2):
-            nc.vector.tensor_tensor(e3[:, halves[h]], e2[:, halves[h]], share[:, halves[h]], ALU.mult)
-        for h in range(2):
-            nc.vector.tensor_tensor(fn[:, halves[h]], e3[:, halves[h]], bn[:, halves[h]], ALU.add)
 
-        nc.vector.tensor_tensor(placed[:].indirect(token_list[:]), fn[:], gate_scaled[:], ALU.mult)
-        for j in range(T // OUT_CHUNK):
-            cols = slice(j * OUT_CHUNK, (j + 1) * OUT_CHUNK)
-            result = wide("result%d" % j, F32, OUT_CHUNK)
-            nc.vector.tensor_tensor(result[:], placed[:, cols], base_chunks[j][:], ALU.add)
+        step_t2(0)
+        step_e(0)
+        step_bn(0)
+        step_n(1)
+        step_bn_run(0)
+        step_dk_run(1)
+        step_e2(0)
+        step_t2(1)
+        step_e3(0)
+        step_e(1)
+        step_fn(0)
+        step_bn(1)
+        gs_first = wide("gs_first", F32, HALF)
+        nc.vector.tensor_tensor(gs_first[:], fn[:, halves[0]], gate_scaled[:, halves[0]], ALU.mult)
+        nc.scalar.activation(placed[:].indirect(token_list[:, list_halves[0]]), gs_first[:], ACT.Copy)
+        step_bn_run(1)
+        step_e2(1)
+        step_e3(1)
+        step_fn(1)
+        nc.vector.tensor_tensor(placed[:].indirect(token_list[:, list_halves[1]]), fn[:, halves[1]], gate_scaled[:, halves[1]], ALU.mult)
+
+        start = 0
+        for j, width in enumerate(OUT_CHUNKS):
+            cols = slice(start, start + width)
+            start = start + width
+            result = wide("result%d" % j, F32, width)
+            nc.vector.tensor_tensor(result[:], placed[:, cols], base_sb[:, cols], ALU.add)
             nc.sync.dma_start(out[:, cols], result[:])

@@ -56,16 +56,16 @@ def tile_attend_hvtilted_oddsof_s_kernel(tc, query, query2, keys_words, keys_sca
         nc.vector.memset(key_scale_pool[:].bitcast(I32), 0)
         nc.vector.memset(val_scale_pool[:].bitcast(I32), 0)
         nc.vector.memset(placed[:], 0.0)
-        consts = sb.tile([P, 4], F32, name="consts")
-        for j, value in enumerate((0.5, 1.0, -0.5, -0.25)):
+        consts = sb.tile([P, 5], F32, name="consts")
+        for j, value in enumerate((0.5, 1.0, -0.5, -0.25, -float(I))):
             nc.gpsimd.memset(consts[:, j:j + 1], value)
-        half_c, one_c, minus_half_c, minus_quarter_c = (consts[:, j:j + 1] for j in range(4))
+        half_c, one_c, minus_half_c, minus_quarter_c, minus_slots_c = (consts[:, j:j + 1] for j in range(5))
 
         note_list = lists.tile([P, I // PER_COLUMN], U16, name="note_list")
         token_list = lists.tile([P, I // PER_COLUMN], U16, name="token_list")
 
         def load_rows(name, src):
-            raw = sb.tile([P, PACK, Q], F32, name=name)
+            raw = sb.tile([P, PACK, Q], F32, name=name, align_bytes=64)
             nc.sync.dma_start(raw[:], src.rearrange("(p j) w -> p j w", j=PACK))
             return raw
 
@@ -116,11 +116,8 @@ def tile_attend_hvtilted_oddsof_s_kernel(tc, query, query2, keys_words, keys_sca
             nc.vector.quantize_mx(out=codes[:].bitcast(FP8X4), scales=scales[:], in_=grouped.rearrange("p w j -> p (w j)"))
             return codes, scales
 
-        def gpsimd_round(dst, src):
-            nc.gpsimd.tensor_scalar(dst, src, 1.0, 0.0, ALU.mult, ALU.add)
-
-        def weave_rows(name, engine_copy, raw):
-            woven = sb.tile([P, Q, PACK], BF16, name=name, align_bytes=64)
+        def weave_rows(name, engine_copy, raw, tag=None):
+            woven = sb.tile([P, Q, PACK], BF16, name=name, tag=tag or name, align_bytes=64)
             weave(engine_copy, woven[:], raw[:])
             return woven
 
@@ -158,28 +155,29 @@ def tile_attend_hvtilted_oddsof_s_kernel(tc, query, query2, keys_words, keys_sca
             nc.vector.tensor_copy(key_words[:, halves[h]], key_word_pool[:].bitcast(U32).indirect(token_list[:, list_halves[h]]))
             a_banks.append(product("a_bank%d" % h, query_q, key_words[:, halves[h]], key_scales[:, halves[h]]))
 
-        dquery_w = weave_rows("dquery_w", gpsimd_round, dquery_raw)
-        gout_w = weave_rows("gout_w", gpsimd_round, gout_raw)
-        reserve_less = column("reserve_less")
-        nc.gpsimd.tensor_scalar(reserve_less[:], reserve_c[:], 1.0, -float(I), ALU.mult, ALU.add)
+        dquery_w = weave_rows("dquery_w", nc.scalar.copy, dquery_raw)
 
         score = wide("score")
-        p = wide("p")
+        p = wide("p", tag="dquery_raw")
         p_run = wide("p_run", F32, G)
         for h in range(2):
             nc.vector.scalar_tensor_tensor(score[:, halves[h]], a_banks[h][:], lam_c[:], gate[:, halves[h]], ALU.subtract, ALU.mult)
             nc.scalar.activation(p[:, halves[h]], score[:, halves[h]], ACT.Exp, bias=lam_c[:])
+        root_run = wide("root_run", F32, G)
+        inv_run = wide("inv_run", F32, G)
+        for h in range(2):
+            nc.vector.tensor_reduce(p_run[:, run_halves[h]], by_run(p[:, halves[h]]), AXIS_X, ALU.add)
+            nc.scalar.activation(root_run[:, run_halves[h]], p_run[:, run_halves[h]], ACT.Abs_reciprocal_sqrt)
+        nc.scalar.activation(inv_run[:], root_run[:], ACT.Square)
+        gout_w = weave_rows("gout_w", nc.scalar.copy, gout_raw, tag="root_run")
         val_scales = wide("val_scales", U8)
         nc.vector.tensor_copy(val_scales[:], val_scale_pool[:].indirect(token_list[:]))
-        nc.vector.tensor_reduce(p_run[:], by_run(p[:]), AXIS_X, ALU.add)
         dquery_q = quantise("dquery", dquery_w[:], Q)
         ta_bank = product("ta_bank", dquery_q, key_words[:], key_scales[:])
-        inv_run = wide("inv_run", F32, G)
+        ts = wide("ts")
+        nc.vector.tensor_tensor(ts[:], ta_bank[:], gate[:], ALU.mult)
         share = wide("share")
-        for h in range(2):
-            nc.vector.reciprocal(inv_run[:, run_halves[h]], p_run[:, run_halves[h]])
-        for h in range(2):
-            nc.vector.tensor_tensor(by_run(share[:, halves[h]]), by_run(p[:, halves[h]]), spread(inv_run[:, run_halves[h]]), ALU.mult)
+        nc.vector.tensor_tensor(by_run(share[:]), by_run(p[:]), spread(inv_run[:]), ALU.mult)
 
         root = wide("root")
         u = wide("u")
@@ -189,12 +187,12 @@ def tile_attend_hvtilted_oddsof_s_kernel(tc, query, query2, keys_words, keys_sca
         total = column("total")
         nc.scalar.activation(root[:], share[:], ACT.Abs_reciprocal_sqrt, bias=one_c, scale=-1.0)
         nc.scalar.activation(u[:], root[:], ACT.Square, accum_out=u_sum[:])
+        reserve_less = column("reserve_less")
+        nc.scalar.activation(reserve_less[:], reserve_c[:], ACT.Identity, bias=minus_slots_c)
         nc.scalar.activation(total[:], u_sum[:], ACT.Identity, bias=reserve_less[:])
         nc.scalar.activation(k_plus[:], u[:], ACT.Square, bias=minus_half_c)
         nc.scalar.activation(k[:], k_plus[:], ACT.Identity, bias=minus_quarter_c)
 
-        ts = wide("ts")
-        nc.vector.tensor_tensor(ts[:], ta_bank[:], gate[:], ALU.mult)
         gout_q = quantise("gout", gout_w[:], Q)
         weighted = wide("weighted")
         val_words = wide("val_words", U32)

@@ -91,10 +91,11 @@ def tile_attend_hvtilted_oddsof_s_kernel(tc, query, query2, keys_words, keys_sca
             for r in range(4):
                 nc.sync.dma_start(pool_tile[r:P:32, :].bitcast(I32), rows[r:16:4, :])
 
+        note_planes = [load_note_plane(0)]
         nc.sync.dma_start(note_list[:], offs2)
-        nc.sync.dma_start(token_list[:], offs)
-        note_planes = [load_note_plane(t) for t in range(PACK)]
+        note_planes += [load_note_plane(t) for t in range(1, PACK)]
         query2_raw = load_rows("query2_raw", query2)
+        nc.sync.dma_start(token_list[:], offs)
         query_raw = load_rows("query_raw", query)
         load_scales(key_scale_pool, keys_scales)
         key_word_pool = load_words("key_word_pool", keys_words)
@@ -177,7 +178,8 @@ def tile_attend_hvtilted_oddsof_s_kernel(tc, query, query2, keys_words, keys_sca
         ts = wide("ts")
         nc.vector.tensor_tensor(ts[:], ta_bank[:], gate[:], ALU.mult)
         share = wide("share")
-        nc.vector.tensor_tensor(by_run(share[:]), by_run(p[:]), spread(inv_run[:]), ALU.mult)
+        for h in range(2):
+            nc.vector.tensor_tensor(by_run(share[:, halves[h]]), by_run(p[:, halves[h]]), spread(inv_run[:, run_halves[h]]), ALU.mult)
 
         root = wide("root")
         u = wide("u")
@@ -216,13 +218,15 @@ def tile_attend_hvtilted_oddsof_s_kernel(tc, query, query2, keys_words, keys_sca
         n_half = wide("n_half")
         dk = wide("dk")
         dk_run = wide("dk_run", F32, G)
-        t2 = wide("t2")
-        e = wide("e")
         bn = wide("bn")
         bn_run = wide("bn_run", F32, G)
         e2 = wide("e2")
-        e3 = wide("e3")
-        fn = wide("fn")
+
+        def runs(cols):
+            return slice(cols.start // RUN, cols.stop // RUN)
+
+        def local(cols):
+            return slice(cols.start % HALF, (cols.stop - 1) % HALF + 1)
 
         def step_n(h):
             nc.vector.scalar_tensor_tensor(n_half[:, halves[h]], u[:, halves[h]], 0.5, z[:, halves[h]], ALU.subtract, ALU.mult)
@@ -230,27 +234,35 @@ def tile_attend_hvtilted_oddsof_s_kernel(tc, query, query2, keys_words, keys_sca
         def step_dk_run(h):
             nc.vector.tensor_reduce(dk_run[:, run_halves[h]], by_run(dk[:, halves[h]]), AXIS_X, ALU.add)
 
-        def step_t2(h):
-            nc.vector.scalar_tensor_tensor(t2[:, halves[h]], n_half[:, halves[h]], kappa[:], dk[:, halves[h]], ALU.subtract, ALU.mult)
+        def step_t2(h, tag):
+            t2 = wide("t2_%d" % h, F32, HALF, tag=tag)
+            nc.vector.scalar_tensor_tensor(t2[:], n_half[:, halves[h]], kappa[:], dk[:, halves[h]], ALU.subtract, ALU.mult)
+            return t2
 
-        def step_e(h):
-            nc.vector.scalar_tensor_tensor(by_run(e[:, halves[h]]), by_run(z[:, halves[h]]), 0.5, spread(dk_run[:, run_halves[h]]), ALU.mult, ALU.mult)
+        def step_e(h, tag):
+            e = wide("e_%d" % h, F32, HALF, tag=tag)
+            nc.vector.scalar_tensor_tensor(by_run(e[:]), by_run(z[:, halves[h]]), 0.5, spread(dk_run[:, run_halves[h]]), ALU.mult, ALU.mult)
+            return e
 
-        def step_bn(h):
-            nc.vector.scalar_tensor_tensor(bn[:, halves[h]], k[:, halves[h]], delta[:], t2[:, halves[h]], ALU.mult, ALU.subtract)
+        def step_bn(cols, t2):
+            nc.vector.scalar_tensor_tensor(bn[:, cols], k[:, cols], delta[:], t2[:, local(cols)], ALU.mult, ALU.subtract)
 
-        def step_bn_run(h):
-            nc.vector.tensor_reduce(bn_run[:, run_halves[h]], by_run(bn[:, halves[h]]), AXIS_X, ALU.add)
+        def step_bn_run(cols):
+            nc.vector.tensor_reduce(bn_run[:, runs(cols)], by_run(bn[:, cols]), AXIS_X, ALU.add)
 
-        def step_e2(h):
-            nc.vector.tensor_tensor(by_run(e2[:, halves[h]]), by_run(e[:, halves[h]]), spread(bn_run[:, run_halves[h]]), ALU.subtract)
+        def finish(h, e):
+            e3 = wide("e3_%d" % h, F32, HALF)
+            fn = wide("fn_%d" % h, F32, HALF)
+            pieces = quarters[2 * h:2 * h + 2]
+            for cols in pieces:
+                nc.vector.tensor_tensor(by_run(e2[:, cols]), by_run(e[:, local(cols)]), spread(bn_run[:, runs(cols)]), ALU.subtract)
+            for cols in pieces:
+                nc.vector.tensor_tensor(e3[:, local(cols)], e2[:, cols], share[:, cols], ALU.mult)
+            for cols in pieces:
+                nc.vector.tensor_tensor(fn[:, local(cols)], e3[:, local(cols)], bn[:, cols], ALU.add)
+            return fn
 
-        def step_e3(h):
-            nc.vector.tensor_tensor(e3[:, halves[h]], e2[:, halves[h]], share[:, halves[h]], ALU.mult)
-
-        def step_fn(h):
-            nc.vector.tensor_tensor(fn[:, halves[h]], e3[:, halves[h]], bn[:, halves[h]], ALU.add)
-
+        quarters = [slice(j * I // 4, (j + 1) * I // 4) for j in range(4)]
         step_n(0)
         tr = wide("tr")
         tr_sum = column("tr_sum")
@@ -272,26 +284,25 @@ def tile_attend_hvtilted_oddsof_s_kernel(tc, query, query2, keys_words, keys_sca
         gate_scaled = wide("gate_scaled")
         nc.scalar.activation(gate_scaled[:], gate[:], ACT.Copy, scale=out_scale[:])
 
-        step_t2(0)
-        step_e(0)
-        step_bn(0)
+        t2_first = step_t2(0, None)
+        e_first = step_e(0, None)
+        step_bn(halves[0], t2_first)
         step_n(1)
-        step_bn_run(0)
+        step_bn_run(halves[0])
         step_dk_run(1)
-        step_e2(0)
-        step_t2(1)
-        step_e3(0)
-        step_e(1)
-        step_fn(0)
-        step_bn(1)
+        fn_first = finish(0, e_first)
         gs_first = wide("gs_first", F32, HALF)
-        nc.vector.tensor_tensor(gs_first[:], fn[:, halves[0]], gate_scaled[:, halves[0]], ALU.mult)
+        for cols in quarters[:2]:
+            nc.vector.tensor_tensor(gs_first[:, cols], fn_first[:, cols], gate_scaled[:, cols], ALU.mult)
         nc.scalar.activation(placed[:].indirect(token_list[:, list_halves[0]]), gs_first[:], ACT.Copy)
-        step_bn_run(1)
-        step_e2(1)
-        step_e3(1)
-        step_fn(1)
-        nc.vector.tensor_tensor(placed[:].indirect(token_list[:, list_halves[1]]), fn[:, halves[1]], gate_scaled[:, halves[1]], ALU.mult)
+        e_second = step_e(1, "e3_0")
+        t2_second = step_t2(1, "fn_0")
+        for cols in quarters[2:]:
+            step_bn(cols, t2_second)
+        for cols in quarters[2:]:
+            step_bn_run(cols)
+        fn_second = finish(1, e_second)
+        nc.vector.tensor_tensor(placed[:].indirect(token_list[:, list_halves[1]]), fn_second[:], gate_scaled[:, halves[1]], ALU.mult)
 
         start = 0
         for j, width in enumerate(OUT_CHUNKS):

@@ -19,7 +19,7 @@ D, E, T, I, Q, U, G = 512, 512, 2048, 512, 128, 1024, 64
 RUN = I // G
 HALF = I // 2
 PER_COLUMN = 16
-OUT_CHUNKS = (640, 576, 512, 320)
+OUT_CHUNKS = (256, 384, 512, 512, 384)
 
 FLOPS = 2 * Q * I * (3 * D + E)
 
@@ -277,14 +277,14 @@ def tile_attend_hvtilted_oddsof_s_kernel(tc, query, query2, keys_words, keys_sca
         dz = wide("dz")
         dz_sum = column("dz_sum")
         nc.vector.scalar_tensor_tensor(dz[:], dk[:], 0.5, z[:], ALU.mult, ALU.mult, accum_out=dz_sum[:])
-        delta = column("delta")
-        nc.scalar.activation(delta[:], dz_sum[:], ACT.Copy, scale=inv_total[:])
         out_scale = column("out_scale")
         nc.scalar.activation(out_scale[:], inv_total[:], ACT.Copy, scale=-1024.0)
         gate_scaled = wide("gate_scaled")
         nc.scalar.activation(gate_scaled[:], gate[:], ACT.Copy, scale=out_scale[:])
 
         t2_first = step_t2(0, None)
+        delta = column("delta")
+        nc.vector.tensor_tensor(delta[:], dz_sum[:], inv_total[:], ALU.mult)
         e_first = step_e(0, None)
         step_bn(halves[0], t2_first)
         step_n(1)

from contextlib import ExitStack

import concourse.mybir as mybir

F32 = mybir.dt.float32
BF16 = mybir.dt.bfloat16
I32 = mybir.dt.int32
U32 = mybir.dt.uint32
U16 = mybir.dt.uint16
U8 = mybir.dt.uint8
FP8X4 = mybir.dt.float8_e4m3fn_x4
ALU = mybir.AluOpType
ACT = mybir.ActivationFunctionType
AXIS_X = mybir.AxisListType.X

P = 128
PACK = 4
D, E, T, I, Q, U, G = 512, 512, 2048, 512, 128, 1024, 64
RUN = I // G
HALF = I // 2
PER_COLUMN = 16
OUT_CHUNKS = (256, 384, 512, 512, 384)

FLOPS = 2 * Q * I * (3 * D + E)

VECTOR_SLOTS = 352


def tile_attend_hvtilted_oddsof_s_kernel(tc, query, query2, keys_words, keys_scales, notes, lam, reserve, gout,
                                          vals_words, vals_scales, dquery, base, offs2, offs, out):
    nc = tc.nc
    with ExitStack() as ctx:
        lists = ctx.enter_context(tc.tile_pool(name="lists", bufs=1))
        sb = ctx.enter_context(tc.tile_pool(name="sb", bufs=1))
        ps = ctx.enter_context(tc.psum_pool(name="ps", bufs=1))

        def wide(name, dtype=F32, columns=I, tag=None):
            return sb.tile([P, columns], dtype, name=name, tag=tag or name, align_bytes=64)

        def column(name):
            return sb.tile([P, 1], F32, name=name)

        halves = [slice(h * HALF, (h + 1) * HALF) for h in range(2)]
        run_halves = [slice(h * G // 2, (h + 1) * G // 2) for h in range(2)]
        list_halves = [slice(h * HALF // PER_COLUMN, (h + 1) * HALF // PER_COLUMN) for h in range(2)]

        def by_run(ap):
            return ap.rearrange("p (g j) -> p g j", j=RUN)

        def spread(ap):
            return ap.unsqueeze(2).to_broadcast([P, ap.shape[1], RUN])

        key_scale_pool = wide("key_scale_pool", U8, T)
        val_scale_pool = wide("val_scale_pool", U8, T)
        placed = wide("placed", F32, T)
        nc.vector.memset(key_scale_pool[:].bitcast(I32), 0)
        nc.vector.memset(val_scale_pool[:].bitcast(I32), 0)
        nc.vector.memset(placed[:], 0.0)
        consts = sb.tile([P, 5], F32, name="consts")
        for j, value in enumerate((0.5, 1.0, -0.5, -0.25, -float(I))):
            nc.gpsimd.memset(consts[:, j:j + 1], value)
        half_c, one_c, minus_half_c, minus_quarter_c, minus_slots_c = (consts[:, j:j + 1] for j in range(5))

        note_list = lists.tile([P, I // PER_COLUMN], U16, name="note_list")
        token_list = lists.tile([P, I // PER_COLUMN], U16, name="token_list")

        def load_rows(name, src):
            raw = sb.tile([P, PACK, Q], F32, name=name, align_bytes=64)
            nc.sync.dma_start(raw[:], src.rearrange("(p j) w -> p j w", j=PACK))
            return raw

        def load_words(name, src):
            words = wide(name, I32, T)
            nc.sync.dma_start(words[:], src[0].rearrange("p n t -> p (n t)").bitcast(I32))
            return words

        def load_column(name, src):
            tile = column(name)
            nc.sync.dma_start(tile[:], src)
            return tile

        note_rows = notes.rearrange("(p j) u -> j p u", j=PACK)

        def load_note_plane(t):
            plane = wide("note_plane%d" % t, F32, U)
            nc.sync.dma_start(plane[:], note_rows[t])
            return plane

        def load_scales(pool_tile, src):
            rows = src[0].bitcast(I32)
            for r in range(4):
                nc.sync.dma_start(pool_tile[r:P:32, :].bitcast(I32), rows[r:16:4, :])

        note_planes = [load_note_plane(0)]
        nc.sync.dma_start(note_list[:], offs2)
        note_planes += [load_note_plane(t) for t in range(1, PACK)]
        query2_raw = load_rows("query2_raw", query2)
        nc.sync.dma_start(token_list[:], offs)
        query_raw = load_rows("query_raw", query)
        load_scales(key_scale_pool, keys_scales)
        key_word_pool = load_words("key_word_pool", keys_words)
        load_scales(val_scale_pool, vals_scales)
        lam_c = load_column("lam_c", lam)
        dquery_raw = load_rows("dquery_raw", dquery)
        gout_raw = load_rows("gout_raw", gout)
        val_word_pool = load_words("val_word_pool", vals_words)
        reserve_c = load_column("reserve_c", reserve)
        base_sb = wide("base_sb", F32, T)
        nc.sync.dma_start(base_sb[:], base)

        def weave(engine_copy, dst, src):
            engine_copy(dst.rearrange("p (c i) t -> p c t i", i=4), src.rearrange("p t (c i) -> p c t i", i=4))

        def quantise(name, grouped, columns):
            codes = wide(name + "_codes", U32, columns)
            scales = wide(name + "_scales", U8, columns)
            nc.vector.quantize_mx(out=codes[:].bitcast(FP8X4), scales=scales[:], in_=grouped.rearrange("p w j -> p (w j)"))
            return codes, scales

        def weave_rows(name, engine_copy, raw, tag=None):
            woven = sb.tile([P, Q, PACK], BF16, name=name, tag=tag or name, align_bytes=64)
            weave(engine_copy, woven[:], raw[:])
            return woven

        def product(name, rows, codes, scales):
            bank = ps.tile([Q, codes.shape[1]], F32, name=name)
            nc.tensor.matmul_mx(out=bank[:], lhsT=rows[0][:].bitcast(FP8X4), lhsT_scale=rows[1][:],
                                rhs=codes.bitcast(FP8X4), rhs_scale=scales, start=True, stop=True)
            return bank

        note_w = sb.tile([P, I, PACK], BF16, name="note_w", align_bytes=64)
        note_g = sb.tile([P, PACK, I - VECTOR_SLOTS], BF16, name="note_g", align_bytes=64)
        cut = VECTOR_SLOTS // PER_COLUMN
        for t in range(PACK):
            nc.vector.tensor_copy(note_w[:, :VECTOR_SLOTS, t], note_planes[t][:].indirect(note_list[:, :cut]))
            nc.scalar.activation(note_g[:, t, :], note_planes[t][:].indirect(note_list[:, cut:]), ACT.Copy)
        weave(nc.scalar.copy, note_w[:, VECTOR_SLOTS:, :], note_g[:])
        query2_w = weave_rows("query2_w", nc.scalar.copy, query2_raw)
        note_codes, note_scales = quantise("note", note_w[:], I)
        query2_q = quantise("query2", query2_w[:], Q)
        b_bank = product("b_bank", query2_q, note_codes[:], note_scales[:])
        query_w = weave_rows("query_w", nc.scalar.copy, query_raw)
        key_scales = wide("key_scales", U8)
        nc.vector.tensor_copy(key_scales[:], key_scale_pool[:].indirect(token_list[:]))
        query_q = quantise("query", query_w[:], Q)

        tanh_b = wide("tanh_b")
        gate = wide("gate")
        for h in range(2):
            nc.scalar.activation(tanh_b[:, halves[h]], b_bank[:, halves[h]], ACT.Tanh, scale=0.5)
            nc.scalar.activation(gate[:, halves[h]], tanh_b[:, halves[h]], ACT.Identity, bias=half_c, scale=0.5)

        key_words = wide("key_words", U32)
        a_banks = []
        for h in range(2):
            nc.vector.tensor_copy(key_words[:, halves[h]], key_word_pool[:].bitcast(U32).indirect(token_list[:, list_halves[h]]))
            a_banks.append(product("a_bank%d" % h, query_q, key_words[:, halves[h]], key_scales[:, halves[h]]))

        dquery_w = weave_rows("dquery_w", nc.scalar.copy, dquery_raw)

        score = wide("score")
        p = wide("p", tag="dquery_raw")
        p_run = wide("p_run", F32, G)
        for h in range(2):
            nc.vector.scalar_tensor_tensor(score[:, halves[h]], a_banks[h][:], lam_c[:], gate[:, halves[h]], ALU.subtract, ALU.mult)
            nc.scalar.activation(p[:, halves[h]], score[:, halves[h]], ACT.Exp, bias=lam_c[:])
        root_run = wide("root_run", F32, G)
        inv_run = wide("inv_run", F32, G)
        for h in range(2):
            nc.vector.tensor_reduce(p_run[:, run_halves[h]], by_run(p[:, halves[h]]), AXIS_X, ALU.add)
            nc.scalar.activation(root_run[:, run_halves[h]], p_run[:, run_halves[h]], ACT.Abs_reciprocal_sqrt)
        nc.scalar.activation(inv_run[:], root_run[:], ACT.Square)
        gout_w = weave_rows("gout_w", nc.scalar.copy, gout_raw, tag="root_run")
        val_scales = wide("val_scales", U8)
        nc.vector.tensor_copy(val_scales[:], val_scale_pool[:].indirect(token_list[:]))
        dquery_q = quantise("dquery", dquery_w[:], Q)
        ta_bank = product("ta_bank", dquery_q, key_words[:], key_scales[:])
        ts = wide("ts")
        nc.vector.tensor_tensor(ts[:], ta_bank[:], gate[:], ALU.mult)
        share = wide("share")
        for h in range(2):
            nc.vector.tensor_tensor(by_run(share[:, halves[h]]), by_run(p[:, halves[h]]), spread(inv_run[:, run_halves[h]]), ALU.mult)

        root = wide("root")
        u = wide("u")
        u_sum = column("u_sum")
        k_plus = wide("k_plus")
        k = wide("k")
        total = column("total")
        nc.scalar.activation(root[:], share[:], ACT.Abs_reciprocal_sqrt, bias=one_c, scale=-1.0)
        nc.scalar.activation(u[:], root[:], ACT.Square, accum_out=u_sum[:])
        reserve_less = column("reserve_less")
        nc.scalar.activation(reserve_less[:], reserve_c[:], ACT.Identity, bias=minus_slots_c)
        nc.scalar.activation(total[:], u_sum[:], ACT.Identity, bias=reserve_less[:])
        nc.scalar.activation(k_plus[:], u[:], ACT.Square, bias=minus_half_c)
        nc.scalar.activation(k[:], k_plus[:], ACT.Identity, bias=minus_quarter_c)

        gout_q = quantise("gout", gout_w[:], Q)
        weighted = wide("weighted")
        val_words = wide("val_words", U32)
        nc.vector.tensor_copy(val_words[:], val_word_pool[:].bitcast(U32).indirect(token_list[:]))
        c_bank = product("c_bank", gout_q, val_words[:], val_scales[:])
        ts_mean = wide("ts_mean", F32, G, tag="val_word_pool")
        for h in range(2):
            nc.vector.tensor_tensor(weighted[:, halves[h]], share[:, halves[h]], ts[:, halves[h]], ALU.mult)
        for h in range(2):
            nc.vector.tensor_reduce(ts_mean[:, run_halves[h]], by_run(weighted[:, halves[h]]), AXIS_X, ALU.add)
        inv_total = column("inv_total")
        nc.vector.reciprocal(inv_total[:], total[:])
        z = wide("z")
        for h in range(2):
            nc.vector.tensor_tensor(by_run(z[:, halves[h]]), by_run(ts[:, halves[h]]), spread(ts_mean[:, run_halves[h]]), ALU.subtract)
        cr = wide("cr")
        cr_sum = column("cr_sum")
        nc.vector.scalar_tensor_tensor(cr[:], u[:], 1.0, c_bank[:], ALU.subtract, ALU.mult, accum_out=cr_sum[:])
        c_mean = column("c_mean")
        nc.scalar.activation(c_mean[:], cr_sum[:], ACT.Copy, scale=inv_total[:])
        n_half = wide("n_half")
        dk = wide("dk")
        dk_run = wide("dk_run", F32, G)
        bn = wide("bn")
        bn_run = wide("bn_run", F32, G)
        e2 = wide("e2")

        def runs(cols):
            return slice(cols.start // RUN, cols.stop // RUN)

        def local(cols):
            return slice(cols.start % HALF, (cols.stop - 1) % HALF + 1)

        def step_n(h):
            nc.vector.scalar_tensor_tensor(n_half[:, halves[h]], u[:, halves[h]], 0.5, z[:, halves[h]], ALU.subtract, ALU.mult)

        def step_dk_run(h):
            nc.vector.tensor_reduce(dk_run[:, run_halves[h]], by_run(dk[:, halves[h]]), AXIS_X, ALU.add)

        def step_t2(h, tag):
            t2 = wide("t2_%d" % h, F32, HALF, tag=tag)
            nc.vector.scalar_tensor_tensor(t2[:], n_half[:, halves[h]], kappa[:], dk[:, halves[h]], ALU.subtract, ALU.mult)
            return t2

        def step_e(h, tag):
            e = wide("e_%d" % h, F32, HALF, tag=tag)
            nc.vector.scalar_tensor_tensor(by_run(e[:]), by_run(z[:, halves[h]]), 0.5, spread(dk_run[:, run_halves[h]]), ALU.mult, ALU.mult)
            return e

        def step_bn(cols, t2):
            nc.vector.scalar_tensor_tensor(bn[:, cols], k[:, cols], delta[:], t2[:, local(cols)], ALU.mult, ALU.subtract)

        def step_bn_run(cols):
            nc.vector.tensor_reduce(bn_run[:, runs(cols)], by_run(bn[:, cols]), AXIS_X, ALU.add)

        def finish(h, e):
            e3 = wide("e3_%d" % h, F32, HALF)
            fn = wide("fn_%d" % h, F32, HALF)
            pieces = quarters[2 * h:2 * h + 2]
            for cols in pieces:
                nc.vector.tensor_tensor(by_run(e2[:, cols]), by_run(e[:, local(cols)]), spread(bn_run[:, runs(cols)]), ALU.subtract)
            for cols in pieces:
                nc.vector.tensor_tensor(e3[:, local(cols)], e2[:, cols], share[:, cols], ALU.mult)
            for cols in pieces:
                nc.vector.tensor_tensor(fn[:, local(cols)], e3[:, local(cols)], bn[:, cols], ALU.add)
            return fn

        quarters = [slice(j * I // 4, (j + 1) * I // 4) for j in range(4)]
        step_n(0)
        tr = wide("tr")
        tr_sum = column("tr_sum")
        nc.vector.scalar_tensor_tensor(tr[:], k_plus[:], 0.25, z[:], ALU.subtract, ALU.mult, accum_out=tr_sum[:])
        half_inv = column("half_inv")
        nc.scalar.activation(half_inv[:], inv_total[:], ACT.Copy, scale=0.5)
        kappa = column("kappa")
        nc.scalar.activation(kappa[:], tr_sum[:], ACT.Copy, scale=half_inv[:])
        for h in range(2):
            nc.vector.scalar_tensor_tensor(dk[:, halves[h]], c_bank[:, halves[h]], c_mean[:], k[:, halves[h]], ALU.subtract, ALU.mult)
        step_dk_run(0)
        dz = wide("dz")
        dz_sum = column("dz_sum")
        nc.vector.scalar_tensor_tensor(dz[:], dk[:], 0.5, z[:], ALU.mult, ALU.mult, accum_out=dz_sum[:])
        out_scale = column("out_scale")
        nc.scalar.activation(out_scale[:], inv_total[:], ACT.Copy, scale=-1024.0)
        gate_scaled = wide("gate_scaled")
        nc.scalar.activation(gate_scaled[:], gate[:], ACT.Copy, scale=out_scale[:])

        t2_first = step_t2(0, None)
        delta = column("delta")
        nc.vector.tensor_tensor(delta[:], dz_sum[:], inv_total[:], ALU.mult)
        e_first = step_e(0, None)
        step_bn(halves[0], t2_first)
        step_n(1)
        step_bn_run(halves[0])
        step_dk_run(1)
        fn_first = finish(0, e_first)
        gs_first = wide("gs_first", F32, HALF)
        for cols in quarters[:2]:
            nc.vector.tensor_tensor(gs_first[:, cols], fn_first[:, cols], gate_scaled[:, cols], ALU.mult)
        nc.scalar.activation(placed[:].indirect(token_list[:, list_halves[0]]), gs_first[:], ACT.Copy)
        e_second = step_e(1, "e3_0")
        t2_second = step_t2(1, "fn_0")
        for cols in quarters[2:]:
            step_bn(cols, t2_second)
        for cols in quarters[2:]:
            step_bn_run(cols)
        fn_second = finish(1, e_second)
        nc.vector.tensor_tensor(placed[:].indirect(token_list[:, list_halves[1]]), fn_second[:], gate_scaled[:, halves[1]], ALU.mult)

        start = 0
        for j, width in enumerate(OUT_CHUNKS):
            cols = slice(start, start + width)
            start = start + width
            result = wide("result%d" % j, F32, width)
            nc.vector.tensor_tensor(result[:], placed[:, cols], base_sb[:, cols], ALU.add)
            nc.sync.dma_start(out[:, cols], result[:])
